import numpy as np
import ml_dtypes


def mxq(x, axis, fmt="e4m3"):
    dtype, down = {"e4m3": (ml_dtypes.float8_e4m3fn, 7), "e5m2": (ml_dtypes.float8_e5m2, 14)}[fmt]
    v = np.moveaxis(np.asarray(x, np.float32).astype(ml_dtypes.bfloat16).astype(np.float64), axis, -1)
    blocks = v.reshape(v.shape[:-1] + (-1, 32))
    amax = np.abs(blocks).max(-1, keepdims=True)
    byte = np.maximum(np.where(amax > 0, np.frexp(amax)[1] - 1 + 127, 0) - down, 1)
    scale = np.exp2(byte - 127.0)
    codes = (blocks / scale).astype(np.float32).astype(dtype).astype(np.float64)
    return np.moveaxis((codes * scale).reshape(v.shape), -1, axis)


WIDE = False


def mx_kscale(k, group=512):
    if not WIDE:
        return np.ones(k)
    levels = np.array([10, -10, 5, -5, 0])
    if group != 512:
        return np.exp2(np.random.permutation(np.resize(levels, k // group))).repeat(group)
    if k % 512:
        return np.exp2(np.random.permutation(np.resize(levels, k // 32))).repeat(32)
    a = np.empty((k // 512, 16))
    for p in range(k // 512):
        a[p, :8] = np.random.permutation(np.resize(levels, 8))
        for g in range(8):
            far = levels[np.abs(levels - a[p, g]) >= 10]
            a[p, g + 8] = far[np.random.randint(len(far))]
    return np.exp2(a.ravel()).repeat(32)


def f64(x):
    return np.asarray(x).astype(np.float64)


def sigmoid(v):
    return 1.0 / (1.0 + np.exp(-v))


G, D, M, O, N = 2, 256, 128, 256, 512


def setup_inputs():
    n = np.random.standard_normal
    s_d = mx_kscale(D, 0)
    s_o = mx_kscale(O, 0)
    return {
        "x": (n((G, D, N)) * s_d[:, None]).astype(np.float32),
        "w1": (n((G, D, M)) / np.sqrt(D) / s_d[:, None]).astype(np.float32),
        "w2": (n((G, D, M)) / np.sqrt(D) / s_d[:, None]).astype(np.float32),
        "st": (np.random.uniform(4.0, 16.0, (G, M, 1))).astype(np.float32),
        "gb": (0.5 * n((G, M, 1))).astype(np.float32),
        "wo": (n((G, O, M)) / np.sqrt(O) / s_o[:, None]).astype(np.float32),
        "dy": (n((G, O, N)) * s_o[:, None]).astype(np.float32),
        "dx": (n((G, D, N)) * s_d[:, None]).astype(np.float32),
        "og": (np.random.uniform(0.5, 2.0, (G, M, 1))).astype(np.float32),
        "base": (0.3 * n((G, M, N))).astype(np.float32),
    }


def reference(x, w1, w2, st, gb, wo, dy, dx, og, base):
    w1q = mxq(f64(w1), 1, "e4m3")
    xq = mxq(f64(x), 1, "e4m3")
    z1 = w1q.transpose(0, 2, 1) @ xq
    dxq = mxq(f64(dx), 1, "e4m3")
    tz1 = w1q.transpose(0, 2, 1) @ dxq
    w2q = mxq(f64(w2), 1, "e4m3")
    z2 = w2q.transpose(0, 2, 1) @ xq
    tz2 = w2q.transpose(0, 2, 1) @ dxq
    mu = np.mean(z1 * z2, axis=-1, keepdims=True)
    gt = sigmoid(mu * f64(st) + f64(gb))
    woq = mxq(f64(wo), 1, "e4m3")
    dyq = mxq(f64(dy), 1, "e4m3")
    c0 = woq.transpose(0, 2, 1) @ dyq
    dgt = np.sum(c0 * z1, axis=-1, keepdims=True)
    dmu = dgt * gt * (1.0 - gt) * f64(st)
    xmu = np.mean(tz1 * z2 + tz2 * z1, axis=-1, keepdims=True)
    xgt = xmu * f64(st) * gt * (1.0 - gt)
    xdgt = np.sum(tz1 * c0, axis=-1, keepdims=True)
    xdmu = ((xdgt * gt + xgt * dgt) * (1.0 - gt) + xgt * (-1.0) * dgt * gt) * f64(st)
    xdz1 = xgt * c0 + xdmu / 512.0 * z2 + tz2 * dmu / 512.0
    y = xdz1 * f64(og) + f64(base)
    return y

@@ -1,0 +1,209 @@
+from contextlib import ExitStack
+
+import concourse.mybir as mybir
+
+G, D, M, N = 2, 256, 128, 512
+FLOPS = 5 * G * 2 * D * M * N
+
+F32 = mybir.dt.float32
+BF16 = mybir.dt.bfloat16
+U32 = mybir.dt.uint32
+U8 = mybir.dt.uint8
+FP8X4 = mybir.dt.float8_e4m3fn_x4
+ALU = mybir.AluOpType
+ACT = mybir.ActivationFunctionType
+
+P = 128
+PACK = 4
+ROWS = D // PACK
+QUAD = 32
+X_VECTOR_COLS = 320
+DX_VECTOR_COLS = 384
+DY_SCALAR_COLS = 256
+
+
+def tile_rows_hvrowgate_kernel(tc, x, w1, w2, st, gb, wo, dy, dx, og, base, out):
+    nc = tc.nc
+    with ExitStack() as ctx:
+        sb = ctx.enter_context(tc.tile_pool(name="sb", bufs=1))
+        psum = ctx.enter_context(tc.psum_pool(name="psum", bufs=1))
+        ctx.enter_context(tc.manual_schedule())
+
+        def load(name, src):
+            width = src.shape[2]
+            raw = sb.tile([P, PACK, width], F32, name=name + "_raw")
+            nc.sync.dma_start(out=raw[:], in_=src.rearrange("g (p j) w -> (g p) j w", j=PACK))
+            grouped = sb.tile([P, width, PACK], BF16, name=name + "_bf16", align_bytes=64)
+            codes = sb.tile([P, width], U32, name=name + "_codes", align_bytes=64)
+            scales = sb.tile([P, width], U8, name=name + "_scales", align_bytes=64)
+            return {"raw": raw, "grouped": grouped, "codes": codes, "scales": scales}
+
+        def views(op, lo, hi):
+            dst = op["grouped"][:, lo:hi, :].rearrange("p (c i) j -> p c j i", i=4)
+            src = op["raw"][:, :, lo:hi].rearrange("p j (c i) -> p c j i", i=4)
+            return dst, src
+
+        def round_vector(op, lo, hi):
+            dst, src = views(op, lo, hi)
+            nc.vector.tensor_copy(out=dst, in_=src)
+
+        def round_scalar(op, lo, hi):
+            dst, src = views(op, lo, hi)
+            nc.scalar.copy(out=dst, in_=src)
+
+        def round_gpsimd(op, lo, hi):
+            dst, src = views(op, lo, hi)
+            nc.gpsimd.tensor_scalar(out=dst, in0=src, scalar1=1.0, scalar2=0.0, op0=ALU.mult, op1=ALU.add)
+
+        def quantize(op):
+            nc.vector.quantize_mx(
+                out=op["codes"][:].bitcast(FP8X4),
+                scales=op["scales"][:],
+                in_=op["grouped"][:].rearrange("p w j -> p (w j)"),
+            )
+
+        def product(bank, g, weights, moving):
+            rows = slice(ROWS * g, ROWS * (g + 1))
+            nc.tensor.matmul_mx(
+                out=bank[:],
+                lhsT=weights["codes"][rows, :].bitcast(FP8X4),
+                lhsT_scale=weights["scales"][rows, :],
+                rhs=moving["codes"][rows, :].bitcast(FP8X4),
+                rhs_scale=moving["scales"][rows, :],
+                start=True,
+                stop=True,
+            )
+
+        def column(name, g):
+            return sb.tile([P, 1], F32, name="%s_%d" % (name, g))
+
+        def wide(name, g):
+            return sb.tile([P, N], F32, name="%s_%d" % (name, g))
+
+        def row_dot(name, g, bank, factor, other):
+            total = column(name, g)
+            terms = wide(name + "_terms", g)
+            nc.vector.scalar_tensor_tensor(
+                out=terms[:], in0=bank[:], scalar=factor, in1=other[:], op0=ALU.mult, op1=ALU.mult, accum_out=total[:]
+            )
+            return total
+
+        def small(name, g, in0, s1, s2, op0, op1):
+            res = column(name, g)
+            nc.gpsimd.tensor_scalar(out=res[:], in0=in0, scalar1=s1, scalar2=s2, op0=op0, op1=op1)
+            return res
+
+        groups = range(G)
+
+        rows_in = sb.tile([P, P], F32, name="rows_in", align_bytes=64)
+        params = sb.tile([P, P], F32, name="params", align_bytes=64)
+        nc.vector.memset(rows_in[:], 0.0)
+
+        xo = load("x", x)
+        w1o = load("w1", w1)
+        w2o = load("w2", w2)
+        for j, vec in enumerate((st, gb, og)):
+            nc.sync.dma_start(
+                out=rows_in[j:P:QUAD, 0 : G * QUAD].rearrange("q (g i) -> q g i", g=G),
+                in_=vec.rearrange("g (q i) o -> q g (i o)", i=QUAD),
+            )
+        dxo = load("dx", dx)
+        woo = load("wo", wo)
+        dyo = load("dy", dy)
+        base_sb = sb.tile([P, G, N], F32, name="base_sb")
+        nc.sync.dma_start(out=base_sb[:], in_=base.rearrange("g m n -> m g n"))
+
+        banks = [[psum.tile([P, N], F32, name="bank_%d_%d" % (g, b)) for b in range(4)] for g in groups]
+        z1 = [banks[g][0] for g in groups]
+        z2 = [banks[g][1] for g in groups]
+        tz1 = [banks[g][2] for g in groups]
+        tz2 = [banks[g][3] for g in groups]
+
+        round_vector(xo, 0, X_VECTOR_COLS)
+        round_scalar(xo, X_VECTOR_COLS, N)
+        round_vector(w1o, 0, M)
+        round_scalar(w2o, 0, M)
+        quantize(xo)
+        quantize(w1o)
+        quantize(w2o)
+        nc.vector.transpose(out=params[:], in_=rows_in[:])
+        st_c = [params[:, QUAD * g : QUAD * g + 1] for g in groups]
+        gb_c = [params[:, QUAD * g + 1 : QUAD * g + 2] for g in groups]
+        og_c = [params[:, QUAD * g + 2 : QUAD * g + 3] for g in groups]
+        st_n = [small("st_n", g, st_c[g], 1.0 / N, 0.0, ALU.mult, ALU.add) for g in groups]
+        gain = [small("gain", g, st_n[g][:], og_c[g], 0.0, ALU.mult, ALU.add) for g in groups]
+        gb_neg = [small("gb_neg", g, gb_c[g], -1.0, 0.0, ALU.mult, ALU.add) for g in groups]
+
+        for g in groups:
+            product(z1[g], g, w1o, xo)
+        for g in groups:
+            product(z2[g], g, w2o, xo)
+        z1s = [wide("z1s", g) for g in groups]
+        for g in groups:
+            nc.scalar.copy(out=z1s[g][:], in_=z1[g][:])
+
+        round_vector(dxo, 0, DX_VECTOR_COLS)
+        round_scalar(dxo, DX_VECTOR_COLS, N)
+        round_scalar(woo, 0, M)
+        arg = [row_dot("arg", 0, z2[0], st_n[0][:], z1s[0])]
+        quantize(dxo)
+        for g in groups:
+            product(tz2[g], g, w2o, dxo)
+        for g in groups:
+            product(tz1[g], g, w1o, dxo)
+        arg.append(row_dot("arg", 1, z2[1], st_n[1][:], z1s[1]))
+        quantize(woo)
+
+        gate, rest = [], []
+        for g in groups:
+            gate.append(column("gate", g))
+            rest.append(column("rest", g))
+            nc.scalar.activation(out=gate[g][:], in_=arg[g][:], func=ACT.Sigmoid, bias=gb_c[g], scale=1.0)
+            nc.scalar.activation(out=rest[g][:], in_=arg[g][:], func=ACT.Sigmoid, bias=gb_neg[g][:], scale=-1.0)
+
+        round_scalar(dyo, 0, DY_SCALAR_COLS)
+        round_gpsimd(dyo, DY_SCALAR_COLS, N)
+        slope = [small("slope", g, gate[g][:], rest[g][:], gain[g][:], ALU.mult, ALU.mult) for g in groups]
+        bend = [small("bend", g, rest[g][:], gate[g][:], st_n[g][:], ALU.subtract, ALU.mult) for g in groups]
+
+        tz1s = [wide("tz1s", g) for g in groups]
+        for g in groups:
+            nc.scalar.copy(out=tz1s[g][:], in_=tz1[g][:])
+        r2 = [row_dot("r2", g, tz2[g], 1.0, z1s[g]) for g in groups]
+        quantize(dyo)
+        c0v, c0a = z1, tz1
+        for g in groups:
+            product(c0v[g], g, woo, dyo)
+        for g in groups:
+            product(c0a[g], g, woo, dyo)
+        r1, a, h = [], [], []
+        for g in groups:
+            r1.append(row_dot("r1", g, z2[g], 1.0, tz1s[g]))
+            a.append(small("a", g, r1[g][:], r2[g][:], slope[g][:], ALU.add, ALU.mult))
+            h.append(small("h", g, r1[g][:], r2[g][:], bend[g][:], ALU.add, ALU.mult))
+
+        first = []
+        for g in groups:
+            scaled = wide("scaled", g)
+            nc.scalar.activation(out=scaled[:], in_=c0a[g][:], func=ACT.Copy, scale=a[g][:])
+            first.append(wide("first", g))
+            nc.gpsimd.tensor_tensor(out=first[g][:], in0=scaled[:], in1=base_sb[:, g, :], op=ALU.add)
+
+        c, e, b = [], [], []
+        for g in groups:
+            c.append(row_dot("c", g, c0v[g], slope[g][:], z1s[g]))
+            e.append(row_dot("e", g, c0v[g], slope[g][:], tz1s[g]))
+            b.append(column("b", g))
+            nc.scalar.activation(out=b[g][:], in_=c[g][:], func=ACT.Identity, bias=e[g][:], scale=h[g][:])
+
+        second = [wide("second", g) for g in groups]
+        for g in groups:
+            nc.vector.scalar_tensor_tensor(
+                out=second[g][:], in0=tz2[g][:], scalar=c[g][:], in1=first[g][:], op0=ALU.mult, op1=ALU.add
+            )
+        for g in groups:
+            result = wide("result", g)
+            nc.vector.scalar_tensor_tensor(
+                out=result[:], in0=z2[g][:], scalar=b[g][:], in1=second[g][:], op0=ALU.mult, op1=ALU.add
+            )
+            nc.sync.dma_start(out=out[g], in_=result[:])

@@ -18,8 +18,8 @@ PACK = 4
 ROWS = D // PACK
 QUAD = 32
 X_VECTOR_COLS = 320
-DX_VECTOR_COLS = 384
-DY_SCALAR_COLS = 256
+DX_VECTOR_COLS = 352
+DY_VECTOR_COLS = 160
 
 
 def tile_rows_hvrowgate_kernel(tc, x, w1, w2, st, gb, wo, dy, dx, og, base, out):
@@ -50,10 +50,6 @@ def tile_rows_hvrowgate_kernel(tc, x, w1, w2, st, gb, wo, dy, dx, og, base, out)
         def round_scalar(op, lo, hi):
             dst, src = views(op, lo, hi)
             nc.scalar.copy(out=dst, in_=src)
-
-        def round_gpsimd(op, lo, hi):
-            dst, src = views(op, lo, hi)
-            nc.gpsimd.tensor_scalar(out=dst, in0=src, scalar1=1.0, scalar2=0.0, op0=ALU.mult, op1=ALU.add)
 
         def quantize(op):
             nc.vector.quantize_mx(
@@ -130,80 +126,89 @@ def tile_rows_hvrowgate_kernel(tc, x, w1, w2, st, gb, wo, dy, dx, og, base, out)
         st_c = [params[:, QUAD * g : QUAD * g + 1] for g in groups]
         gb_c = [params[:, QUAD * g + 1 : QUAD * g + 2] for g in groups]
         og_c = [params[:, QUAD * g + 2 : QUAD * g + 3] for g in groups]
-        st_n = [small("st_n", g, st_c[g], 1.0 / N, 0.0, ALU.mult, ALU.add) for g in groups]
-        gain = [small("gain", g, st_n[g][:], og_c[g], 0.0, ALU.mult, ALU.add) for g in groups]
-        gb_neg = [small("gb_neg", g, gb_c[g], -1.0, 0.0, ALU.mult, ALU.add) for g in groups]
+        st_n = [small("st_n", g, st_c[g], -1.0 / N, 0.0, ALU.mult, ALU.add) for g in groups]
+        gb_half = [small("gb_half", g, gb_c[g], -0.5, 0.0, ALU.mult, ALU.add) for g in groups]
+        gain = [small("gain", g, st_n[g][:], og_c[g], 0.25, ALU.mult, ALU.mult) for g in groups]
 
-        for g in groups:
-            product(z1[g], g, w1o, xo)
-        for g in groups:
-            product(z2[g], g, w2o, xo)
         z1s = [wide("z1s", g) for g in groups]
         for g in groups:
-            nc.scalar.copy(out=z1s[g][:], in_=z1[g][:])
-
+            product(z1[g], g, w1o, xo)
+            product(z2[g], g, w2o, xo)
+        nc.scalar.copy(out=z1s[0][:], in_=z1[0][:])
         round_vector(dxo, 0, DX_VECTOR_COLS)
         round_scalar(dxo, DX_VECTOR_COLS, N)
+        nc.scalar.copy(out=z1s[1][:], in_=z1[1][:])
         round_scalar(woo, 0, M)
-        arg = [row_dot("arg", 0, z2[0], st_n[0][:], z1s[0])]
         quantize(dxo)
-        for g in groups:
-            product(tz2[g], g, w2o, dxo)
-        for g in groups:
-            product(tz1[g], g, w1o, dxo)
-        arg.append(row_dot("arg", 1, z2[1], st_n[1][:], z1s[1]))
+        product(tz2[0], 0, w2o, dxo)
+        product(tz1[1], 1, w1o, dxo)
+        product(tz1[0], 0, w1o, dxo)
+        product(tz2[1], 1, w2o, dxo)
+        arg = [row_dot("arg", g, z2[g], st_n[g][:], z1s[g]) for g in groups]
         quantize(woo)
 
-        gate, rest = [], []
-        for g in groups:
-            gate.append(column("gate", g))
-            rest.append(column("rest", g))
-            nc.scalar.activation(out=gate[g][:], in_=arg[g][:], func=ACT.Sigmoid, bias=gb_c[g], scale=1.0)
-            nc.scalar.activation(out=rest[g][:], in_=arg[g][:], func=ACT.Sigmoid, bias=gb_neg[g][:], scale=-1.0)
-
-        round_scalar(dyo, 0, DY_SCALAR_COLS)
-        round_gpsimd(dyo, DY_SCALAR_COLS, N)
-        slope = [small("slope", g, gate[g][:], rest[g][:], gain[g][:], ALU.mult, ALU.mult) for g in groups]
-        bend = [small("bend", g, rest[g][:], gate[g][:], st_n[g][:], ALU.subtract, ALU.mult) for g in groups]
-
-        tz1s = [wide("tz1s", g) for g in groups]
-        for g in groups:
-            nc.scalar.copy(out=tz1s[g][:], in_=tz1[g][:])
+        round_vector(dyo, 0, DY_VECTOR_COLS)
+        round_scalar(dyo, DY_VECTOR_COLS, N)
         r2 = [row_dot("r2", g, tz2[g], 1.0, z1s[g]) for g in groups]
         quantize(dyo)
-        c0v, c0a = z1, tz1
+        c0 = z1
         for g in groups:
-            product(c0v[g], g, woo, dyo)
-        for g in groups:
-            product(c0a[g], g, woo, dyo)
-        r1, a, h = [], [], []
-        for g in groups:
-            r1.append(row_dot("r1", g, z2[g], 1.0, tz1s[g]))
-            a.append(small("a", g, r1[g][:], r2[g][:], slope[g][:], ALU.add, ALU.mult))
-            h.append(small("h", g, r1[g][:], r2[g][:], bend[g][:], ALU.add, ALU.mult))
+            product(c0[g], g, woo, dyo)
 
-        first = []
+        tz1s = [wide("tz1s", g) for g in groups]
+        nc.scalar.copy(out=tz1s[1][:], in_=tz1[1][:])
+        tilt = [column("tilt", g) for g in groups]
+        tilt_sq = [column("tilt_sq", g) for g in groups]
         for g in groups:
+            nc.scalar.activation(out=tilt[g][:], in_=arg[g][:], func=ACT.Tanh, bias=gb_half[g][:], scale=0.5)
+        for g in groups:
+            nc.scalar.activation(out=tilt_sq[g][:], in_=tilt[g][:], func=ACT.Square)
+        nc.scalar.copy(out=tz1s[0][:], in_=tz1[0][:])
+        slope = [small("slope", g, tilt_sq[g][:], -1.0, gain[g][:], ALU.add, ALU.mult) for g in groups]
+        bend = [small("bend", g, tilt[g][:], st_n[g][:], -1.0, ALU.mult, ALU.mult) for g in groups]
+
+        a, h, r1 = {}, {}, {}
+        for g in (1, 0):
+            r1[g] = row_dot("r1", g, z2[g], 1.0, tz1s[g])
+            a[g] = small("a", g, r1[g][:], r2[g][:], slope[g][:], ALU.add, ALU.mult)
+        for g in groups:
+            h[g] = small("h", g, r1[g][:], r2[g][:], bend[g][:], ALU.add, ALU.mult)
+
+        first, c, b = {}, {}, {}
+
+        def first_terms(g):
             scaled = wide("scaled", g)
-            nc.scalar.activation(out=scaled[:], in_=c0a[g][:], func=ACT.Copy, scale=a[g][:])
-            first.append(wide("first", g))
+            nc.scalar.activation(out=scaled[:], in_=c0[g][:], func=ACT.Copy, scale=a[g][:])
+            first[g] = wide("first", g)
             nc.gpsimd.tensor_tensor(out=first[g][:], in0=scaled[:], in1=base_sb[:, g, :], op=ALU.add)
 
-        c, e, b = [], [], []
-        for g in groups:
-            c.append(row_dot("c", g, c0v[g], slope[g][:], z1s[g]))
-            e.append(row_dot("e", g, c0v[g], slope[g][:], tz1s[g]))
-            b.append(column("b", g))
-            nc.scalar.activation(out=b[g][:], in_=c[g][:], func=ACT.Identity, bias=e[g][:], scale=h[g][:])
+        def dy_sums(g):
+            c[g] = row_dot("c", g, c0[g], slope[g][:], z1s[g])
+            return row_dot("e", g, c0[g], slope[g][:], tz1s[g])
 
-        second = [wide("second", g) for g in groups]
-        for g in groups:
-            nc.vector.scalar_tensor_tensor(
-                out=second[g][:], in0=tz2[g][:], scalar=c[g][:], in1=first[g][:], op0=ALU.mult, op1=ALU.add
-            )
-        for g in groups:
+        def last_factor(g, e):
+            b[g] = column("b", g)
+            nc.scalar.activation(out=b[g][:], in_=c[g][:], func=ACT.Identity, bias=e[:], scale=h[g][:])
+
+        first_terms(1)
+        e0 = dy_sums(0)
+        first_terms(0)
+        last_factor(0, e0)
+        last_factor(1, dy_sums(1))
+
+        halves = (slice(0, N // 2), slice(N // 2, N))
+        for g in (1, 0):
+            second = wide("second", g)
             result = wide("result", g)
-            nc.vector.scalar_tensor_tensor(
-                out=result[:], in0=z2[g][:], scalar=b[g][:], in1=second[g][:], op0=ALU.mult, op1=ALU.add
-            )
-            nc.sync.dma_start(out=out[g], in_=result[:])
+            for cols in halves:
+                nc.vector.scalar_tensor_tensor(
+                    out=second[:, cols], in0=tz2[g][:, cols], scalar=c[g][:], in1=first[g][:, cols], op0=ALU.mult, op1=ALU.add
+                )
+            for cols in halves:
+                nc.vector.scalar_tensor_tensor(
+                    out=result[:, cols], in0=z2[g][:, cols], scalar=b[g][:], in1=second[:, cols], op0=ALU.mult, op1=ALU.add
+                )
+                if g == 0:
+                    nc.sync.dma_start(out=out[g][:, cols], in_=result[:, cols])
+            if g == 1:
+                nc.sync.dma_start(out=out[g], in_=result[:])

@@ -17,9 +17,9 @@ P = 128
 PACK = 4
 ROWS = D // PACK
 QUAD = 32
-X_VECTOR_COLS = 320
-DX_VECTOR_COLS = 352
-DY_VECTOR_COLS = 160
+X_VECTOR_COLS = 368
+DX_VECTOR_COLS = 384
+DY_SCALAR_COLS = 384
 
 
 def tile_rows_hvrowgate_kernel(tc, x, w1, w2, st, gb, wo, dy, dx, og, base, out):
@@ -50,6 +50,10 @@ def tile_rows_hvrowgate_kernel(tc, x, w1, w2, st, gb, wo, dy, dx, og, base, out)
         def round_scalar(op, lo, hi):
             dst, src = views(op, lo, hi)
             nc.scalar.copy(out=dst, in_=src)
+
+        def round_gpsimd(op, lo, hi):
+            dst, src = views(op, lo, hi)
+            nc.gpsimd.tensor_scalar(out=dst, in0=src, scalar1=1.0, scalar2=0.0, op0=ALU.mult, op1=ALU.add)
 
         def quantize(op):
             nc.vector.quantize_mx(
@@ -104,8 +108,8 @@ def tile_rows_hvrowgate_kernel(tc, x, w1, w2, st, gb, wo, dy, dx, og, base, out)
                 in_=vec.rearrange("g (q i) o -> q g (i o)", i=QUAD),
             )
         dxo = load("dx", dx)
-        woo = load("wo", wo)
         dyo = load("dy", dy)
+        woo = load("wo", wo)
         base_sb = sb.tile([P, G, N], F32, name="base_sb")
         nc.sync.dma_start(out=base_sb[:], in_=base.rearrange("g m n -> m g n"))
 
@@ -138,29 +142,29 @@ def tile_rows_hvrowgate_kernel(tc, x, w1, w2, st, gb, wo, dy, dx, og, base, out)
         round_vector(dxo, 0, DX_VECTOR_COLS)
         round_scalar(dxo, DX_VECTOR_COLS, N)
         nc.scalar.copy(out=z1s[1][:], in_=z1[1][:])
-        round_scalar(woo, 0, M)
         quantize(dxo)
         product(tz2[0], 0, w2o, dxo)
+        product(tz2[1], 1, w2o, dxo)
         product(tz1[1], 1, w1o, dxo)
         product(tz1[0], 0, w1o, dxo)
-        product(tz2[1], 1, w2o, dxo)
         arg = [row_dot("arg", g, z2[g], st_n[g][:], z1s[g]) for g in groups]
-        quantize(woo)
 
-        round_vector(dyo, 0, DY_VECTOR_COLS)
-        round_scalar(dyo, DY_VECTOR_COLS, N)
+        round_scalar(dyo, 0, DY_SCALAR_COLS)
+        round_gpsimd(dyo, DY_SCALAR_COLS, N)
         r2 = [row_dot("r2", g, tz2[g], 1.0, z1s[g]) for g in groups]
+        round_vector(woo, 0, M)
         quantize(dyo)
+        quantize(woo)
         c0 = z1
         for g in groups:
             product(c0[g], g, woo, dyo)
 
         tz1s = [wide("tz1s", g) for g in groups]
-        nc.scalar.copy(out=tz1s[1][:], in_=tz1[1][:])
         tilt = [column("tilt", g) for g in groups]
         tilt_sq = [column("tilt_sq", g) for g in groups]
         for g in groups:
             nc.scalar.activation(out=tilt[g][:], in_=arg[g][:], func=ACT.Tanh, bias=gb_half[g][:], scale=0.5)
+        nc.scalar.copy(out=tz1s[1][:], in_=tz1[1][:])
         for g in groups:
             nc.scalar.activation(out=tilt_sq[g][:], in_=tilt[g][:], func=ACT.Square)
         nc.scalar.copy(out=tz1s[0][:], in_=tz1[0][:])
@@ -176,11 +180,14 @@ def tile_rows_hvrowgate_kernel(tc, x, w1, w2, st, gb, wo, dy, dx, og, base, out)
 
         first, c, b = {}, {}, {}
 
-        def first_terms(g):
+        halves = (slice(0, N // 2), slice(N // 2, N))
+
+        def first_terms(g, pieces):
             scaled = wide("scaled", g)
             nc.scalar.activation(out=scaled[:], in_=c0[g][:], func=ACT.Copy, scale=a[g][:])
             first[g] = wide("first", g)
-            nc.gpsimd.tensor_tensor(out=first[g][:], in0=scaled[:], in1=base_sb[:, g, :], op=ALU.add)
+            for cols in pieces:
+                nc.gpsimd.tensor_tensor(out=first[g][:, cols], in0=scaled[:, cols], in1=base_sb[:, g, cols], op=ALU.add)
 
         def dy_sums(g):
             c[g] = row_dot("c", g, c0[g], slope[g][:], z1s[g])
@@ -190,13 +197,12 @@ def tile_rows_hvrowgate_kernel(tc, x, w1, w2, st, gb, wo, dy, dx, og, base, out)
             b[g] = column("b", g)
             nc.scalar.activation(out=b[g][:], in_=c[g][:], func=ACT.Identity, bias=e[:], scale=h[g][:])
 
-        first_terms(1)
+        first_terms(1, (slice(0, N),))
         e0 = dy_sums(0)
-        first_terms(0)
+        first_terms(0, halves)
         last_factor(0, e0)
         last_factor(1, dy_sums(1))
 
-        halves = (slice(0, N // 2), slice(N // 2, N))
         for g in (1, 0):
             second = wide("second", g)
             result = wide("result", g)

@@ -39,8 +39,8 @@ def tile_rows_hvrowgate_kernel(tc, x, w1, w2, st, gb, wo, dy, dx, og, base, out)
             return {"raw": raw, "grouped": grouped, "codes": codes, "scales": scales}
 
         def views(op, lo, hi):
-            dst = op["grouped"][:, lo:hi, :].rearrange("p (c i) j -> p c j i", i=4)
-            src = op["raw"][:, :, lo:hi].rearrange("p j (c i) -> p c j i", i=4)
+            dst = op["grouped"][:, lo:hi, :].rearrange("p (c i) j -> p c j i", i=2)
+            src = op["raw"][:, :, lo:hi].rearrange("p j (c i) -> p c j i", i=2)
             return dst, src
 
         def round_vector(op, lo, hi):
@@ -127,13 +127,23 @@ def tile_rows_hvrowgate_kernel(tc, x, w1, w2, st, gb, wo, dy, dx, og, base, out)
         quantize(w1o)
         quantize(w2o)
         nc.vector.transpose(out=params[:], in_=rows_in[:])
-        st_c = [params[:, QUAD * g : QUAD * g + 1] for g in groups]
-        gb_c = [params[:, QUAD * g + 1 : QUAD * g + 2] for g in groups]
-        og_c = [params[:, QUAD * g + 2 : QUAD * g + 3] for g in groups]
-        st_n = [small("st_n", g, st_c[g], -1.0 / N, 0.0, ALU.mult, ALU.add) for g in groups]
-        gb_half = [small("gb_half", g, gb_c[g], -0.5, 0.0, ALU.mult, ALU.add) for g in groups]
-        gain = [small("gain", g, st_n[g][:], og_c[g], 0.25, ALU.mult, ALU.mult) for g in groups]
+        st_c, gb_c, og_c = (params[:, j : G * QUAD : QUAD] for j in range(3))
 
+        def scaled_param(name, vec, factor):
+            res = sb.tile([P, G], F32, name=name)
+            nc.vector.tensor_scalar(out=res[:], in0=vec, scalar1=factor, scalar2=None, op0=ALU.mult)
+            return res
+
+        def gain_param(name, factor):
+            res = sb.tile([P, G], F32, name=name)
+            nc.vector.scalar_tensor_tensor(out=res[:], in0=st_c, scalar=factor, in1=og_c, op0=ALU.mult, op1=ALU.mult)
+            return res
+
+        st_pos = scaled_param("st_pos", st_c, 1.0 / N)
+        st_neg = scaled_param("st_neg", st_c, -1.0 / N)
+        gb_half = scaled_param("gb_half", gb_c, 0.5)
+        gain_pos = gain_param("gain_pos", 0.25 / N)
+        gain_neg = gain_param("gain_neg", -0.25 / N)
         z1s = [wide("z1s", g) for g in groups]
         for g in groups:
             product(z1[g], g, w1o, xo)
@@ -147,7 +157,7 @@ def tile_rows_hvrowgate_kernel(tc, x, w1, w2, st, gb, wo, dy, dx, og, base, out)
         product(tz2[1], 1, w2o, dxo)
         product(tz1[1], 1, w1o, dxo)
         product(tz1[0], 0, w1o, dxo)
-        arg = [row_dot("arg", g, z2[g], st_n[g][:], z1s[g]) for g in groups]
+        arg = [row_dot("arg", g, z2[g], st_pos[:, g : g + 1], z1s[g]) for g in groups]
 
         round_scalar(dyo, 0, DY_SCALAR_COLS)
         round_gpsimd(dyo, DY_SCALAR_COLS, N)
@@ -162,14 +172,20 @@ def tile_rows_hvrowgate_kernel(tc, x, w1, w2, st, gb, wo, dy, dx, og, base, out)
         tz1s = [wide("tz1s", g) for g in groups]
         tilt = [column("tilt", g) for g in groups]
         tilt_sq = [column("tilt_sq", g) for g in groups]
+        slope = [column("slope", g) for g in groups]
+        bend = [column("bend", g) for g in groups]
         for g in groups:
-            nc.scalar.activation(out=tilt[g][:], in_=arg[g][:], func=ACT.Tanh, bias=gb_half[g][:], scale=0.5)
-        nc.scalar.copy(out=tz1s[1][:], in_=tz1[1][:])
-        for g in groups:
+            nc.scalar.activation(out=tilt[g][:], in_=arg[g][:], func=ACT.Tanh, bias=gb_half[:, g : g + 1], scale=0.5)
+        for g in (1, 0):
+            nc.scalar.copy(out=tz1s[g][:], in_=tz1[g][:])
+        for g in (1, 0):
             nc.scalar.activation(out=tilt_sq[g][:], in_=tilt[g][:], func=ACT.Square)
-        nc.scalar.copy(out=tz1s[0][:], in_=tz1[0][:])
-        slope = [small("slope", g, tilt_sq[g][:], -1.0, gain[g][:], ALU.add, ALU.mult) for g in groups]
-        bend = [small("bend", g, tilt[g][:], st_n[g][:], -1.0, ALU.mult, ALU.mult) for g in groups]
+        for g in (1, 0):
+            nc.scalar.activation(out=bend[g][:], in_=tilt[g][:], func=ACT.Copy, scale=st_neg[:, g : g + 1])
+        for g in (1, 0):
+            nc.scalar.activation(
+                out=slope[g][:], in_=tilt_sq[g][:], func=ACT.Identity, scale=gain_neg[:, g : g + 1], bias=gain_pos[:, g : g + 1]
+            )
 
         a, h, r1 = {}, {}, {}
         for g in (1, 0):

@@ -17,9 +17,12 @@ P = 128
 PACK = 4
 ROWS = D // PACK
 QUAD = 32
+PAIR = 2
+BANKS = 4
+
 X_VECTOR_COLS = 368
 DX_VECTOR_COLS = 384
-DY_SCALAR_COLS = 384
+DY_SCALAR_COLS = 320
 
 
 def tile_rows_hvrowgate_kernel(tc, x, w1, w2, st, gb, wo, dy, dx, og, base, out):
@@ -38,28 +41,28 @@ def tile_rows_hvrowgate_kernel(tc, x, w1, w2, st, gb, wo, dy, dx, og, base, out)
             scales = sb.tile([P, width], U8, name=name + "_scales", align_bytes=64)
             return {"raw": raw, "grouped": grouped, "codes": codes, "scales": scales}
 
-        def views(op, lo, hi):
-            dst = op["grouped"][:, lo:hi, :].rearrange("p (c i) j -> p c j i", i=2)
-            src = op["raw"][:, :, lo:hi].rearrange("p j (c i) -> p c j i", i=2)
+        def views(operand, lo, hi):
+            dst = operand["grouped"][:, lo:hi, :].rearrange("p (c i) j -> p c j i", i=PAIR)
+            src = operand["raw"][:, :, lo:hi].rearrange("p j (c i) -> p c j i", i=PAIR)
             return dst, src
 
-        def round_vector(op, lo, hi):
-            dst, src = views(op, lo, hi)
+        def round_vector(operand, lo, hi):
+            dst, src = views(operand, lo, hi)
             nc.vector.tensor_copy(out=dst, in_=src)
 
-        def round_scalar(op, lo, hi):
-            dst, src = views(op, lo, hi)
+        def round_scalar(operand, lo, hi):
+            dst, src = views(operand, lo, hi)
             nc.scalar.copy(out=dst, in_=src)
 
-        def round_gpsimd(op, lo, hi):
-            dst, src = views(op, lo, hi)
+        def round_gpsimd(operand, lo, hi):
+            dst, src = views(operand, lo, hi)
             nc.gpsimd.tensor_scalar(out=dst, in0=src, scalar1=1.0, scalar2=0.0, op0=ALU.mult, op1=ALU.add)
 
-        def quantize(op):
+        def quantize(operand):
             nc.vector.quantize_mx(
-                out=op["codes"][:].bitcast(FP8X4),
-                scales=op["scales"][:],
-                in_=op["grouped"][:].rearrange("p w j -> p (w j)"),
+                out=operand["codes"][:].bitcast(FP8X4),
+                scales=operand["scales"][:],
+                in_=operand["grouped"][:].rearrange("p w j -> p (w j)"),
             )
 
         def product(bank, g, weights, moving):
@@ -88,12 +91,15 @@ def tile_rows_hvrowgate_kernel(tc, x, w1, w2, st, gb, wo, dy, dx, og, base, out)
             )
             return total
 
-        def small(name, g, in0, s1, s2, op0, op1):
+        def sum_times(name, g, left, right, factor):
             res = column(name, g)
-            nc.gpsimd.tensor_scalar(out=res[:], in0=in0, scalar1=s1, scalar2=s2, op0=op0, op1=op1)
+            nc.gpsimd.tensor_scalar(
+                out=res[:], in0=left[:], scalar1=right[:], scalar2=factor[:], op0=ALU.add, op1=ALU.mult
+            )
             return res
 
         groups = range(G)
+        finishing_order = (1, 0)
 
         rows_in = sb.tile([P, P], F32, name="rows_in", align_bytes=64)
         params = sb.tile([P, P], F32, name="params", align_bytes=64)
@@ -113,11 +119,12 @@ def tile_rows_hvrowgate_kernel(tc, x, w1, w2, st, gb, wo, dy, dx, og, base, out)
         base_sb = sb.tile([P, G, N], F32, name="base_sb")
         nc.sync.dma_start(out=base_sb[:], in_=base.rearrange("g m n -> m g n"))
 
-        banks = [[psum.tile([P, N], F32, name="bank_%d_%d" % (g, b)) for b in range(4)] for g in groups]
+        banks = [[psum.tile([P, N], F32, name="bank_%d_%d" % (g, i)) for i in range(BANKS)] for g in groups]
         z1 = [banks[g][0] for g in groups]
         z2 = [banks[g][1] for g in groups]
         tz1 = [banks[g][2] for g in groups]
         tz2 = [banks[g][3] for g in groups]
+        c0 = z1
 
         round_vector(xo, 0, X_VECTOR_COLS)
         round_scalar(xo, X_VECTOR_COLS, N)
@@ -126,6 +133,7 @@ def tile_rows_hvrowgate_kernel(tc, x, w1, w2, st, gb, wo, dy, dx, og, base, out)
         quantize(xo)
         quantize(w1o)
         quantize(w2o)
+
         nc.vector.transpose(out=params[:], in_=rows_in[:])
         st_c, gb_c, og_c = (params[:, j : G * QUAD : QUAD] for j in range(3))
 
@@ -144,6 +152,7 @@ def tile_rows_hvrowgate_kernel(tc, x, w1, w2, st, gb, wo, dy, dx, og, base, out)
         gb_half = scaled_param("gb_half", gb_c, 0.5)
         gain_pos = gain_param("gain_pos", 0.25 / N)
         gain_neg = gain_param("gain_neg", -0.25 / N)
+
         z1s = [wide("z1s", g) for g in groups]
         for g in groups:
             product(z1[g], g, w1o, xo)
@@ -152,11 +161,12 @@ def tile_rows_hvrowgate_kernel(tc, x, w1, w2, st, gb, wo, dy, dx, og, base, out)
         round_vector(dxo, 0, DX_VECTOR_COLS)
         round_scalar(dxo, DX_VECTOR_COLS, N)
         nc.scalar.copy(out=z1s[1][:], in_=z1[1][:])
+
         quantize(dxo)
-        product(tz2[0], 0, w2o, dxo)
-        product(tz2[1], 1, w2o, dxo)
-        product(tz1[1], 1, w1o, dxo)
-        product(tz1[0], 0, w1o, dxo)
+        for g in groups:
+            product(tz2[g], g, w2o, dxo)
+        for g in finishing_order:
+            product(tz1[g], g, w1o, dxo)
         arg = [row_dot("arg", g, z2[g], st_pos[:, g : g + 1], z1s[g]) for g in groups]
 
         round_scalar(dyo, 0, DY_SCALAR_COLS)
@@ -165,7 +175,6 @@ def tile_rows_hvrowgate_kernel(tc, x, w1, w2, st, gb, wo, dy, dx, og, base, out)
         round_vector(woo, 0, M)
         quantize(dyo)
         quantize(woo)
-        c0 = z1
         for g in groups:
             product(c0[g], g, woo, dyo)
 
@@ -176,26 +185,30 @@ def tile_rows_hvrowgate_kernel(tc, x, w1, w2, st, gb, wo, dy, dx, og, base, out)
         bend = [column("bend", g) for g in groups]
         for g in groups:
             nc.scalar.activation(out=tilt[g][:], in_=arg[g][:], func=ACT.Tanh, bias=gb_half[:, g : g + 1], scale=0.5)
-        for g in (1, 0):
+        for g in finishing_order:
             nc.scalar.copy(out=tz1s[g][:], in_=tz1[g][:])
-        for g in (1, 0):
+        for g in finishing_order:
             nc.scalar.activation(out=tilt_sq[g][:], in_=tilt[g][:], func=ACT.Square)
-        for g in (1, 0):
+        for g in finishing_order:
             nc.scalar.activation(out=bend[g][:], in_=tilt[g][:], func=ACT.Copy, scale=st_neg[:, g : g + 1])
-        for g in (1, 0):
+        for g in finishing_order:
             nc.scalar.activation(
-                out=slope[g][:], in_=tilt_sq[g][:], func=ACT.Identity, scale=gain_neg[:, g : g + 1], bias=gain_pos[:, g : g + 1]
+                out=slope[g][:],
+                in_=tilt_sq[g][:],
+                func=ACT.Identity,
+                scale=gain_neg[:, g : g + 1],
+                bias=gain_pos[:, g : g + 1],
             )
 
         a, h, r1 = {}, {}, {}
-        for g in (1, 0):
+        for g in finishing_order:
             r1[g] = row_dot("r1", g, z2[g], 1.0, tz1s[g])
-            a[g] = small("a", g, r1[g][:], r2[g][:], slope[g][:], ALU.add, ALU.mult)
+            a[g] = sum_times("a", g, r1[g], r2[g], slope[g])
         for g in groups:
-            h[g] = small("h", g, r1[g][:], r2[g][:], bend[g][:], ALU.add, ALU.mult)
+            h[g] = sum_times("h", g, r1[g], r2[g], bend[g])
 
         first, c, b = {}, {}, {}
-
+        whole = (slice(0, N),)
         halves = (slice(0, N // 2), slice(N // 2, N))
 
         def first_terms(g, pieces):
@@ -213,24 +226,35 @@ def tile_rows_hvrowgate_kernel(tc, x, w1, w2, st, gb, wo, dy, dx, og, base, out)
             b[g] = column("b", g)
             nc.scalar.activation(out=b[g][:], in_=c[g][:], func=ACT.Identity, bias=e[:], scale=h[g][:])
 
-        first_terms(1, (slice(0, N),))
-        e0 = dy_sums(0)
-        first_terms(0, halves)
-        last_factor(0, e0)
-        last_factor(1, dy_sums(1))
+        early, late = finishing_order
+        first_terms(early, whole)
+        e_late = dy_sums(late)
+        first_terms(late, halves)
+        last_factor(late, e_late)
+        last_factor(early, dy_sums(early))
 
-        for g in (1, 0):
+        for g in finishing_order:
             second = wide("second", g)
             result = wide("result", g)
             for cols in halves:
                 nc.vector.scalar_tensor_tensor(
-                    out=second[:, cols], in0=tz2[g][:, cols], scalar=c[g][:], in1=first[g][:, cols], op0=ALU.mult, op1=ALU.add
+                    out=second[:, cols],
+                    in0=tz2[g][:, cols],
+                    scalar=c[g][:],
+                    in1=first[g][:, cols],
+                    op0=ALU.mult,
+                    op1=ALU.add,
                 )
             for cols in halves:
                 nc.vector.scalar_tensor_tensor(
-                    out=result[:, cols], in0=z2[g][:, cols], scalar=b[g][:], in1=second[:, cols], op0=ALU.mult, op1=ALU.add
+                    out=result[:, cols],
+                    in0=z2[g][:, cols],
+                    scalar=b[g][:],
+                    in1=second[:, cols],
+                    op0=ALU.mult,
+                    op1=ALU.add,
                 )
-                if g == 0:
+                if g == late:
                     nc.sync.dma_start(out=out[g][:, cols], in_=result[:, cols])
-            if g == 1:
+            if g == early:
                 nc.sync.dma_start(out=out[g], in_=result[:])

from contextlib import ExitStack

import concourse.mybir as mybir

G, D, M, N = 2, 256, 128, 512
FLOPS = 5 * G * 2 * D * M * N

F32 = mybir.dt.float32
BF16 = mybir.dt.bfloat16
U32 = mybir.dt.uint32
U8 = mybir.dt.uint8
FP8X4 = mybir.dt.float8_e4m3fn_x4
ALU = mybir.AluOpType
ACT = mybir.ActivationFunctionType

P = 128
PACK = 4
ROWS = D // PACK
QUAD = 32
PAIR = 2
BANKS = 4

X_VECTOR_COLS = 368
DX_VECTOR_COLS = 384
DY_SCALAR_COLS = 320


def tile_rows_hvrowgate_kernel(tc, x, w1, w2, st, gb, wo, dy, dx, og, base, out):
    nc = tc.nc
    with ExitStack() as ctx:
        sb = ctx.enter_context(tc.tile_pool(name="sb", bufs=1))
        psum = ctx.enter_context(tc.psum_pool(name="psum", bufs=1))
        ctx.enter_context(tc.manual_schedule())

        def load(name, src):
            width = src.shape[2]
            raw = sb.tile([P, PACK, width], F32, name=name + "_raw")
            nc.sync.dma_start(out=raw[:], in_=src.rearrange("g (p j) w -> (g p) j w", j=PACK))
            grouped = sb.tile([P, width, PACK], BF16, name=name + "_bf16", align_bytes=64)
            codes = sb.tile([P, width], U32, name=name + "_codes", align_bytes=64)
            scales = sb.tile([P, width], U8, name=name + "_scales", align_bytes=64)
            return {"raw": raw, "grouped": grouped, "codes": codes, "scales": scales}

        def views(operand, lo, hi):
            dst = operand["grouped"][:, lo:hi, :].rearrange("p (c i) j -> p c j i", i=PAIR)
            src = operand["raw"][:, :, lo:hi].rearrange("p j (c i) -> p c j i", i=PAIR)
            return dst, src

        def round_vector(operand, lo, hi):
            dst, src = views(operand, lo, hi)
            nc.vector.tensor_copy(out=dst, in_=src)

        def round_scalar(operand, lo, hi):
            dst, src = views(operand, lo, hi)
            nc.scalar.copy(out=dst, in_=src)

        def round_gpsimd(operand, lo, hi):
            dst, src = views(operand, lo, hi)
            nc.gpsimd.tensor_scalar(out=dst, in0=src, scalar1=1.0, scalar2=0.0, op0=ALU.mult, op1=ALU.add)

        def quantize(operand):
            nc.vector.quantize_mx(
                out=operand["codes"][:].bitcast(FP8X4),
                scales=operand["scales"][:],
                in_=operand["grouped"][:].rearrange("p w j -> p (w j)"),
            )

        def product(bank, g, weights, moving):
            rows = slice(ROWS * g, ROWS * (g + 1))
            nc.tensor.matmul_mx(
                out=bank[:],
                lhsT=weights["codes"][rows, :].bitcast(FP8X4),
                lhsT_scale=weights["scales"][rows, :],
                rhs=moving["codes"][rows, :].bitcast(FP8X4),
                rhs_scale=moving["scales"][rows, :],
                start=True,
                stop=True,
            )

        def column(name, g):
            return sb.tile([P, 1], F32, name="%s_%d" % (name, g))

        def wide(name, g):
            return sb.tile([P, N], F32, name="%s_%d" % (name, g))

        def row_dot(name, g, bank, factor, other):
            total = column(name, g)
            terms = wide(name + "_terms", g)
            nc.vector.scalar_tensor_tensor(
                out=terms[:], in0=bank[:], scalar=factor, in1=other[:], op0=ALU.mult, op1=ALU.mult, accum_out=total[:]
            )
            return total

        def sum_times(name, g, left, right, factor):
            res = column(name, g)
            nc.gpsimd.tensor_scalar(
                out=res[:], in0=left[:], scalar1=right[:], scalar2=factor[:], op0=ALU.add, op1=ALU.mult
            )
            return res

        groups = range(G)
        finishing_order = (1, 0)

        rows_in = sb.tile([P, P], F32, name="rows_in", align_bytes=64)
        params = sb.tile([P, P], F32, name="params", align_bytes=64)
        nc.vector.memset(rows_in[:], 0.0)

        xo = load("x", x)
        w1o = load("w1", w1)
        w2o = load("w2", w2)
        for j, vec in enumerate((st, gb, og)):
            nc.sync.dma_start(
                out=rows_in[j:P:QUAD, 0 : G * QUAD].rearrange("q (g i) -> q g i", g=G),
                in_=vec.rearrange("g (q i) o -> q g (i o)", i=QUAD),
            )
        dxo = load("dx", dx)
        dyo = load("dy", dy)
        woo = load("wo", wo)
        base_sb = sb.tile([P, G, N], F32, name="base_sb")
        nc.sync.dma_start(out=base_sb[:], in_=base.rearrange("g m n -> m g n"))

        banks = [[psum.tile([P, N], F32, name="bank_%d_%d" % (g, i)) for i in range(BANKS)] for g in groups]
        z1 = [banks[g][0] for g in groups]
        z2 = [banks[g][1] for g in groups]
        tz1 = [banks[g][2] for g in groups]
        tz2 = [banks[g][3] for g in groups]
        c0 = z1

        round_vector(xo, 0, X_VECTOR_COLS)
        round_scalar(xo, X_VECTOR_COLS, N)
        round_vector(w1o, 0, M)
        round_scalar(w2o, 0, M)
        quantize(xo)
        quantize(w1o)
        quantize(w2o)

        nc.vector.transpose(out=params[:], in_=rows_in[:])
        st_c, gb_c, og_c = (params[:, j : G * QUAD : QUAD] for j in range(3))

        def scaled_param(name, vec, factor):
            res = sb.tile([P, G], F32, name=name)
            nc.vector.tensor_scalar(out=res[:], in0=vec, scalar1=factor, scalar2=None, op0=ALU.mult)
            return res

        def gain_param(name, factor):
            res = sb.tile([P, G], F32, name=name)
            nc.vector.scalar_tensor_tensor(out=res[:], in0=st_c, scalar=factor, in1=og_c, op0=ALU.mult, op1=ALU.mult)
            return res

        st_pos = scaled_param("st_pos", st_c, 1.0 / N)
        st_neg = scaled_param("st_neg", st_c, -1.0 / N)
        gb_half = scaled_param("gb_half", gb_c, 0.5)
        gain_pos = gain_param("gain_pos", 0.25 / N)
        gain_neg = gain_param("gain_neg", -0.25 / N)

        z1s = [wide("z1s", g) for g in groups]
        for g in groups:
            product(z1[g], g, w1o, xo)
            product(z2[g], g, w2o, xo)
        nc.scalar.copy(out=z1s[0][:], in_=z1[0][:])
        round_vector(dxo, 0, DX_VECTOR_COLS)
        round_scalar(dxo, DX_VECTOR_COLS, N)
        nc.scalar.copy(out=z1s[1][:], in_=z1[1][:])

        quantize(dxo)
        for g in groups:
            product(tz2[g], g, w2o, dxo)
        for g in finishing_order:
            product(tz1[g], g, w1o, dxo)
        arg = [row_dot("arg", g, z2[g], st_pos[:, g : g + 1], z1s[g]) for g in groups]

        round_scalar(dyo, 0, DY_SCALAR_COLS)
        round_gpsimd(dyo, DY_SCALAR_COLS, N)
        r2 = [row_dot("r2", g, tz2[g], 1.0, z1s[g]) for g in groups]
        round_vector(woo, 0, M)
        quantize(dyo)
        quantize(woo)
        for g in groups:
            product(c0[g], g, woo, dyo)

        tz1s = [wide("tz1s", g) for g in groups]
        tilt = [column("tilt", g) for g in groups]
        tilt_sq = [column("tilt_sq", g) for g in groups]
        slope = [column("slope", g) for g in groups]
        bend = [column("bend", g) for g in groups]
        for g in groups:
            nc.scalar.activation(out=tilt[g][:], in_=arg[g][:], func=ACT.Tanh, bias=gb_half[:, g : g + 1], scale=0.5)
        for g in finishing_order:
            nc.scalar.copy(out=tz1s[g][:], in_=tz1[g][:])
        for g in finishing_order:
            nc.scalar.activation(out=tilt_sq[g][:], in_=tilt[g][:], func=ACT.Square)
        for g in finishing_order:
            nc.scalar.activation(out=bend[g][:], in_=tilt[g][:], func=ACT.Copy, scale=st_neg[:, g : g + 1])
        for g in finishing_order:
            nc.scalar.activation(
                out=slope[g][:],
                in_=tilt_sq[g][:],
                func=ACT.Identity,
                scale=gain_neg[:, g : g + 1],
                bias=gain_pos[:, g : g + 1],
            )

        a, h, r1 = {}, {}, {}
        for g in finishing_order:
            r1[g] = row_dot("r1", g, z2[g], 1.0, tz1s[g])
            a[g] = sum_times("a", g, r1[g], r2[g], slope[g])
        for g in groups:
            h[g] = sum_times("h", g, r1[g], r2[g], bend[g])

        first, c, b = {}, {}, {}
        whole = (slice(0, N),)
        halves = (slice(0, N // 2), slice(N // 2, N))

        def first_terms(g, pieces):
            scaled = wide("scaled", g)
            nc.scalar.activation(out=scaled[:], in_=c0[g][:], func=ACT.Copy, scale=a[g][:])
            first[g] = wide("first", g)
            for cols in pieces:
                nc.gpsimd.tensor_tensor(out=first[g][:, cols], in0=scaled[:, cols], in1=base_sb[:, g, cols], op=ALU.add)

        def dy_sums(g):
            c[g] = row_dot("c", g, c0[g], slope[g][:], z1s[g])
            return row_dot("e", g, c0[g], slope[g][:], tz1s[g])

        def last_factor(g, e):
            b[g] = column("b", g)
            nc.scalar.activation(out=b[g][:], in_=c[g][:], func=ACT.Identity, bias=e[:], scale=h[g][:])

        early, late = finishing_order
        first_terms(early, whole)
        e_late = dy_sums(late)
        first_terms(late, halves)
        last_factor(late, e_late)
        last_factor(early, dy_sums(early))

        for g in finishing_order:
            second = wide("second", g)
            result = wide("result", g)
            for cols in halves:
                nc.vector.scalar_tensor_tensor(
                    out=second[:, cols],
                    in0=tz2[g][:, cols],
                    scalar=c[g][:],
                    in1=first[g][:, cols],
                    op0=ALU.mult,
                    op1=ALU.add,
                )
            for cols in halves:
                nc.vector.scalar_tensor_tensor(
                    out=result[:, cols],
                    in0=z2[g][:, cols],
                    scalar=b[g][:],
                    in1=second[:, cols],
                    op0=ALU.mult,
                    op1=ALU.add,
                )
                if g == late:
                    nc.sync.dma_start(out=out[g][:, cols], in_=result[:, cols])
            if g == early:
                nc.sync.dma_start(out=out[g], in_=result[:])
